import numpy as np
import ml_dtypes


def mxq(x, axis, fmt="e4m3"):
    dtype, down = {"e4m3": (ml_dtypes.float8_e4m3fn, 7), "e5m2": (ml_dtypes.float8_e5m2, 14)}[fmt]
    v = np.moveaxis(np.asarray(x, np.float32).astype(ml_dtypes.bfloat16).astype(np.float64), axis, -1)
    blocks = v.reshape(v.shape[:-1] + (-1, 32))
    amax = np.abs(blocks).max(-1, keepdims=True)
    byte = np.maximum(np.where(amax > 0, np.frexp(amax)[1] - 1 + 127, 0) - down, 1)
    scale = np.exp2(byte - 127.0)
    codes = (blocks / scale).astype(np.float32).astype(dtype).astype(np.float64)
    return np.moveaxis((codes * scale).reshape(v.shape), -1, axis)


WIDE = False


def mx_kscale(k):
    if not WIDE:
        return np.ones(k)
    levels = np.array([10, -10, 5, -5, 0])
    if k % 512:
        return np.exp2(np.random.permutation(np.resize(levels, k // 32))).repeat(32)
    a = np.empty((k // 512, 16))
    for p in range(k // 512):
        a[p, :8] = np.random.permutation(np.resize(levels, 8))
        for g in range(8):
            far = levels[np.abs(levels - a[p, g]) >= 10]
            a[p, g + 8] = far[np.random.randint(len(far))]
    return np.exp2(a.ravel()).repeat(32)


def f64(x):
    return np.asarray(x).astype(np.float64)


def striped(idx):
    return np.tile(idx.reshape(-1, 16).T, (8, 1)).astype(np.uint16)


def unstriped(offs):
    return offs[:16].T.reshape(-1).astype(np.int64)


def striped8(idx):
    return np.concatenate([x.reshape(-1, 16).T for x in idx]).astype(np.uint16)


def runs(offs, k):
    lists = np.stack([offs[16 * r : 16 * r + 16].T.reshape(-1) for r in range(8)]).astype(np.int64)
    return lists[np.arange(k) % 512 // 64]


def pack_weight(w):
    k, n = w.shape
    w = f64(np.asarray(w, np.float32).astype(ml_dtypes.bfloat16)).reshape(k // 32, 32, n)
    amax = np.abs(w).max(1)
    byte = np.clip(np.where(amax > 0, np.frexp(amax)[1] - 1 + 127 - 7, 1), 1, 254)
    scaled = (w * np.exp2(127.0 - byte)[:, None, :]).reshape(k, n).astype(np.float32)
    words = np.ascontiguousarray(scaled.reshape(k // 512, 128, 4, n).transpose(0, 1, 3, 2)).astype(ml_dtypes.float8_e4m3fn).view(np.uint8)
    return words, np.ascontiguousarray(byte.astype(np.uint8).reshape(k // 512, 16, n))


def unpack_weight(words, scales):
    g, p, n, _ = words.shape
    vals = np.ascontiguousarray(words).view(ml_dtypes.float8_e4m3fn).astype(np.float64) * np.repeat(np.exp2(scales.astype(np.float64) - 127.0), 8, axis=1)[..., None]
    return vals.transpose(0, 1, 3, 2).reshape(g * 512, n)

def planes(y):
    n, m = y.shape
    v = y.astype(np.float32).astype(ml_dtypes.bfloat16).astype(np.float64).reshape(n // 32, 32, m)
    top = np.abs(v).max(1)
    byte = np.clip(np.where(top > 0, np.frexp(top)[1] - 1 + 127 - 7, 1), 1, 254)
    codes = (v * np.exp2(127.0 - byte)[:, None, :]).reshape(n, m).astype(np.float32).astype(ml_dtypes.float8_e4m3fn).view(np.uint8)
    words = codes.reshape(n // 512, 128, 4, m).transpose(0, 1, 3, 2)
    return np.ascontiguousarray(words), np.ascontiguousarray(byte.astype(np.uint8).reshape(n // 512, 16, m))


K, T, S, N, H = 512, 2048, 512, 512, 512


def setup_inputs():
    n = np.random.standard_normal
    s = mx_kscale(K)[:, None]
    u = mx_kscale(H)
    packed_xT = pack_weight(n((K, T)) * s)
    packed_w1 = pack_weight(n((K, H)) / np.sqrt(K) / s)
    packed_w2 = pack_weight(n((H, N)) / np.sqrt(H) / u[:, None])
    return {
        "x_words": packed_xT[0],
        "x_scales": packed_xT[1],
        "w1_words": packed_w1[0],
        "w1_scales": packed_w1[1],
        "cst": np.random.uniform(0.0, 1.5, (H, S)).astype(np.float32),
        "gn": (np.random.uniform(0.5, 1.5, (H, 1)) * u[:, None]).astype(np.float32),
        "w2_words": packed_w2[0],
        "w2_scales": packed_w2[1],
        "res": (2 * n((N, S))).astype(np.float32),
        "offs": striped(np.random.permutation(T)[:S]),
        "di": striped8(np.stack([np.random.permutation(S) for _ in range(8)])),
        "dj": striped8(np.stack([np.random.permutation(S) for _ in range(8)])),
        "dk": striped8(np.stack([np.random.permutation(S) for _ in range(8)])),
    }


def reference(x_words, x_scales, w1_words, w1_scales, cst, gn, w2_words, w2_scales, res, offs, di, dj, dk):
    xq = unpack_weight(x_words, x_scales)[:, unstriped(offs)]
    y = unpack_weight(w1_words, w1_scales).T @ xq
    z = f64(gn) * (f64(cst) - (np.log(np.exp(-1.0 * (y[np.arange(H)[:, None], runs(di, H)])) + np.exp(-1.0 * (y[np.arange(H)[:, None], runs(dj, H)])) + np.exp(-1.0 * (y[np.arange(H)[:, None], runs(dk, H)])))))
    out_0 = f64(res) + (unpack_weight(w2_words, w2_scales).T @ mxq(z, 0, "e4m3"))
    return (out_0,) + planes(out_0)

@@ -1,0 +1,239 @@
+from contextlib import ExitStack
+
+import concourse.mybir as mybir
+from concourse.masks import make_identity
+
+K, T, S, N, H = 512, 2048, 512, 512, 512
+FLOPS = 2 * K * H * S + 2 * H * N * S
+
+F32 = mybir.dt.float32
+BF16 = mybir.dt.bfloat16
+I32 = mybir.dt.int32
+U32 = mybir.dt.uint32
+U16 = mybir.dt.uint16
+U8 = mybir.dt.uint8
+FP8X4 = mybir.dt.float8_e4m3fn_x4
+ALU = mybir.AluOpType
+ACT = mybir.ActivationFunctionType
+
+P = 128
+PACK = 4
+BLOCK = 128
+CHUNKS = ((0, 256), (256, 512))
+
+
+def tile_picked_softdtw_none_po_kernel(
+    tc, x_words, x_scales, w1_words, w1_scales, cst, gn, w2_words, w2_scales, res, offs, di, dj, dk, out_0, out_1, out_2
+):
+    nc = tc.nc
+    with ExitStack() as ctx:
+        keep = ctx.enter_context(tc.tile_pool(name="keep", bufs=1))
+        ring = ctx.enter_context(tc.tile_pool(name="ring", bufs=2))
+        psum = ctx.enter_context(tc.psum_pool(name="psum", bufs=4))
+
+        def load_scale_rows(queues, plane, scales):
+            rows = scales[0].bitcast(I32)
+            for q, queue in enumerate(queues):
+                queue.dma_start(out=plane[32 * q : 32 * q + 4, :].bitcast(I32), in_=rows[4 * q : 4 * q + 4, :])
+
+        def load_words(tile, words):
+            nc.sync.dma_start(out=tile[:], in_=words[0].rearrange("p n t -> p (n t)").bitcast(I32))
+
+        def deal(words, plane, name):
+            dealt_words = keep.tile([P, PACK, P], I32, name=name + "_dealt_words", align_bytes=64)
+            dealt_plane = keep.tile([P, PACK, P], U8, name=name + "_dealt_plane", align_bytes=64)
+            nc.vector.tensor_copy(out=dealt_words[:], in_=words[:].rearrange("p (m t) -> p t m", t=PACK))
+            nc.vector.tensor_copy(out=dealt_plane[:], in_=plane[:].rearrange("p (m t) -> p t m", t=PACK))
+            return dealt_words, dealt_plane
+
+        x_plane = keep.tile([P, T], U8, name="x_plane", align_bytes=64)
+        w1_plane = keep.tile([P, H], U8, name="w1_plane", tag="w_plane", align_bytes=64)
+        nc.vector.memset(x_plane[:].bitcast(I32), 0)
+        nc.gpsimd.memset(w1_plane[:].bitcast(I32), 0)
+
+        lists = {}
+        for name, source in (("offs", offs), ("di", di), ("dj", dj), ("dk", dk)):
+            lists[name] = keep.tile([P, S // 16], U16, name="list_" + name)
+            nc.sync.dma_start(lists[name][:], source)
+        load_scale_rows([nc.scalar] * 4, x_plane, x_scales)
+        x_raw = keep.tile([P, T], I32, name="x_raw", tag="big_a", align_bytes=64)
+        load_words(x_raw, x_words)
+        w1_raw = keep.tile([P, H], I32, name="w1_raw", tag="big_b", align_bytes=64)
+        load_words(w1_raw, w1_words)
+        load_scale_rows([nc.sync, nc.sync, nc.gpsimd, nc.gpsimd], w1_plane, w1_scales)
+        gain = keep.tile([P, PACK], F32, name="gain")
+        nc.gpsimd.dma_start(out=gain[:], in_=gn.rearrange("(p t) o -> p (t o)", t=PACK))
+
+        ident = keep.tile([P, P], F32, name="ident")
+        make_identity(nc, ident[:])
+
+        warm = keep.tile([P, 1], F32, name="warm")
+        nc.scalar.activation(out=warm[:], in_=ident[:, 0:1], func=ACT.Exp)
+
+        w1_dealt, w1_dealt_plane = deal(w1_raw, w1_plane, "w1")
+
+        w2_plane = keep.tile([P, N], U8, name="w2_plane", tag="w_plane", align_bytes=64)
+        nc.gpsimd.memset(w2_plane[:].bitcast(I32), 0)
+        w2_raw = keep.tile([P, N], I32, name="w2_raw", tag="big_b", align_bytes=64)
+        load_words(w2_raw, w2_words)
+        load_scale_rows([nc.sync] * 4, w2_plane, w2_scales)
+
+        picked_plane = keep.tile([P, S], U8, name="picked_plane", align_bytes=64)
+        nc.vector.tensor_copy(out=picked_plane[:], in_=x_plane[:].indirect(lists["offs"][:]))
+        picked_words = keep.tile([P, S], U32, name="picked_words", align_bytes=64)
+        half = S // 2
+        for h in range(2):
+            nc.vector.tensor_copy(
+                out=picked_words[:, h * half : (h + 1) * half],
+                in_=x_raw[:].bitcast(U32).indirect(lists["offs"][:, h * half // 16 : (h + 1) * half // 16]),
+            )
+
+        y = []
+        for t in range(PACK):
+            bank = psum.tile([P, S], F32, name="y_bank", tag="short")
+            for h in range(2):
+                cols = slice(h * half, (h + 1) * half)
+                nc.tensor.matmul_mx(
+                    out=bank[:, cols],
+                    lhsT=w1_dealt[:, t, :].bitcast(FP8X4),
+                    lhsT_scale=w1_dealt_plane[:, t, :],
+                    rhs=picked_words[:, cols].bitcast(FP8X4),
+                    rhs_scale=picked_plane[:, cols],
+                    start=True,
+                    stop=True,
+                )
+            window = keep.tile([P, S], F32, name=f"y{t}")
+            nc.scalar.copy(out=window[:], in_=bank[:])
+            y.append(window)
+
+        w2_dealt, w2_dealt_plane = deal(w2_raw, w2_plane, "w2")
+
+        cost = keep.tile([P, PACK, S], F32, name="cost", tag="big_a", align_bytes=64)
+        nc.sync.dma_start(out=cost[:], in_=cst.rearrange("(p t) j -> p t j", t=PACK))
+        residual = keep.tile([P, PACK, S], F32, name="residual", tag="big_b", align_bytes=64)
+        nc.sync.dma_start(out=residual[:], in_=res.rearrange("(p t) j -> p t j", t=PACK))
+
+        gain_bank = psum.tile([P, PACK, P], F32, name="gain_bank", tag="base")
+        for t in range(PACK):
+            nc.tensor.transpose(gain_bank[:, t, :], gain[:, t : t + 1].to_broadcast([P, P]), ident[:])
+        gain_row = keep.tile([P, H], F32, name="gain_row")
+        nc.scalar.copy(
+            out=gain_row[:].rearrange("j (u p e) -> j u p e", u=2, e=2),
+            in_=gain_bank[:].rearrange("j (u e) p -> j u p e", u=2),
+        )
+
+        out_words = keep.tile([P, S], I32, name="out_words", align_bytes=64)
+        out_plane = keep.tile([P, S], U8, name="out_plane", align_bytes=64)
+        out_rows = out_0.rearrange("(p t) j -> p t j", t=PACK)
+
+        def add_transposed(bank, term, cols, slots, first=False, last=False):
+            for t in range(slots.start, slots.stop):
+                nc.tensor.matmul(
+                    bank[:, t, :], term[:, t, cols], ident[:],
+                    start=(first and t == 0), stop=(last and t == PACK - 1), is_transpose=True,
+                )
+
+        def look_up(lo, hi):
+            width = hi - lo
+            names = ("first", "step", "low", "third", "gap", "gap3", "far", "near_w", "far_w")
+            v = {name: ring.tile([P, PACK, width], F32, name=name) for name in names}
+            cols = slice(lo // 16, hi // 16)
+            pairs = (slice(0, 2), slice(2, 4))
+            blocks = [slice(j, j + BLOCK) for j in range(0, width, BLOCK)]
+            bases = [psum.tile([P, PACK, P], F32, name="base", tag="base") for b in blocks]
+            sums = [psum.tile([P, PACK, P], F32, name="sums", tag="short") for b in blocks]
+            for base, b in zip(bases, blocks):
+                add_transposed(base, cost[:, :, lo:hi], b, slice(0, PACK), first=True)
+            for t in range(PACK):
+                nc.vector.tensor_copy(out=v["first"][:, t, :], in_=y[t][:].indirect(lists["di"][:, cols]))
+            for t in range(PACK):
+                nc.vector.tensor_tensor(v["step"][:, t, :], y[t][:].indirect(lists["dj"][:, cols]), v["first"][:, t, :], ALU.subtract)
+            for s in pairs:
+                nc.vector.scalar_tensor_tensor(v["low"][:, s, :], v["step"][:, s, :], 0.0, v["first"][:, s, :], ALU.min, ALU.add)
+                nc.scalar.activation(out=v["gap"][:, s, :], in_=v["step"][:, s, :], func=ACT.Abs)
+                for base, b in zip(bases, blocks):
+                    add_transposed(base, v["low"], b, s)
+                    add_transposed(base, v["gap"], b, s)
+            for t in range(PACK):
+                nc.vector.tensor_tensor(v["third"][:, t, :], y[t][:].indirect(lists["dk"][:, cols]), v["low"][:, t, :], ALU.subtract)
+            for s in pairs:
+                nc.vector.scalar_tensor_tensor(v["far"][:, s, :], v["third"][:, s, :], 0.0, v["gap"][:, s, :], ALU.min, ALU.subtract)
+                nc.scalar.activation(out=v["gap3"][:, s, :], in_=v["third"][:, s, :], func=ACT.Abs)
+                nc.scalar.activation(out=v["near_w"][:, s, :], in_=v["gap3"][:, s, :], func=ACT.Exp, scale=-1.0)
+                nc.scalar.activation(out=v["far_w"][:, s, :], in_=v["far"][:, s, :], func=ACT.Exp)
+                for bank, b in zip(sums, blocks):
+                    add_transposed(bank, v["near_w"], b, s, first=True)
+                for bank, b in zip(sums, blocks):
+                    add_transposed(bank, v["far_w"], b, s, last=True)
+                for base, b in zip(bases, blocks):
+                    add_transposed(base, v["far"], b, s, last=True)
+            return bases, sums
+
+        def log_sums(lo, bases, sums):
+            pieces = []
+            for n, (base, bank) in enumerate(zip(bases, sums)):
+                logs = ring.tile([P, H], F32, name="logs", bufs=4)
+                nc.scalar.activation(
+                    out=logs[:].rearrange("j (u p e) -> j u p e", u=2, e=2),
+                    in_=bank[:].rearrange("j (u e) p -> j u p e", u=2),
+                    func=ACT.Ln,
+                    bias=1.0,
+                )
+                pieces.append((lo + n * BLOCK, base, logs))
+            return pieces
+
+        def second_layer(j0, base, logs):
+            cols = slice(j0, j0 + BLOCK)
+            soft = ring.tile([P, H], F32, name="soft")
+            nc.vector.tensor_tensor(
+                soft[:].rearrange("j (u p e) -> j u p e", u=2, e=2),
+                base[:].rearrange("j (u e) p -> j u p e", u=2),
+                logs[:].rearrange("j (u p e) -> j u p e", u=2, e=2),
+                ALU.subtract,
+            )
+            z_rows = ring.tile([P, H], BF16, name="z_rows")
+            nc.vector.tensor_tensor(z_rows[:], soft[:], gain_row[:], ALU.mult)
+            pair_bank = psum.tile([P, 2, BLOCK], F32, name="pair_bank", tag="short")
+            for u in range(2):
+                nc.tensor.transpose(pair_bank[:, u, :], z_rows[:].bitcast(F32)[:, u * P : (u + 1) * P], ident[:])
+            z_grouped = ring.tile([P, BLOCK * PACK], BF16, name="z_grouped", align_bytes=64)
+            nc.scalar.copy(
+                out=z_grouped[:].bitcast(F32).rearrange("p (j u) -> p j u", u=2),
+                in_=pair_bank[:].rearrange("p u j -> p j u"),
+            )
+            z_words = ring.tile([P, BLOCK], U32, name="z_words", align_bytes=64)
+            z_plane = ring.tile([P, BLOCK], U8, name="z_plane", align_bytes=64)
+            nc.vector.quantize_mx(out=z_words[:].bitcast(FP8X4), scales=z_plane[:], in_=z_grouped[:])
+            acc = psum.tile([P, PACK, BLOCK], F32, name="acc", tag="short")
+            for t in range(PACK):
+                nc.tensor.matmul_mx(
+                    out=acc[:, t, :],
+                    lhsT=w2_dealt[:, t, :].bitcast(FP8X4),
+                    lhsT_scale=w2_dealt_plane[:, t, :],
+                    rhs=z_words[:].bitcast(FP8X4),
+                    rhs_scale=z_plane[:],
+                    start=True,
+                    stop=True,
+                )
+            result = ring.tile([P, PACK, BLOCK], F32, name="result", bufs=4)
+            nc.vector.tensor_tensor(result[:], acc[:], residual[:, :, cols], ALU.add)
+            nc.sync.dma_start(out=out_rows[:, :, cols], in_=result[:])
+            grouped = ring.tile([P, BLOCK * PACK], BF16, name="grouped", align_bytes=64)
+            nc.scalar.copy(
+                out=grouped[:].rearrange("p (c i t) -> p c t i", i=4, t=PACK),
+                in_=result[:].rearrange("p t (c i) -> p c t i", i=4),
+            )
+            nc.vector.quantize_mx(out=out_words[:, cols].bitcast(FP8X4), scales=out_plane[:, cols], in_=grouped[:])
+
+        words_out = out_1[0].rearrange("p n t -> p (n t)").bitcast(I32)
+        logged = []
+        for lo, hi in CHUNKS:
+            logged.append(log_sums(lo, *look_up(lo, hi)))
+        for (lo, hi), pieces in zip(CHUNKS, logged):
+            for piece in pieces:
+                second_layer(*piece)
+            nc.sync.dma_start(out=words_out[:, lo:hi], in_=out_words[:, lo:hi])
+        scale_rows = out_2[0].bitcast(I32)
+        for q in range(4):
+            queue = (nc.sync, nc.scalar)[q % 2]
+            queue.dma_start(out=scale_rows[4 * q : 4 * q + 4, :], in_=out_plane[32 * q : 32 * q + 4, :].bitcast(I32))

@@ -31,20 +31,18 @@ def tile_picked_softdtw_none_po_kernel(
         ring = ctx.enter_context(tc.tile_pool(name="ring", bufs=2))
         psum = ctx.enter_context(tc.psum_pool(name="psum", bufs=4))
 
-        def load_scale_rows(queues, plane, scales):
+        def load_scale_rows(queue, plane, scales, quadrants):
             rows = scales[0].bitcast(I32)
-            for q, queue in enumerate(queues):
+            for q in quadrants:
                 queue.dma_start(out=plane[32 * q : 32 * q + 4, :].bitcast(I32), in_=rows[4 * q : 4 * q + 4, :])
 
         def load_words(tile, words):
             nc.sync.dma_start(out=tile[:], in_=words[0].rearrange("p n t -> p (n t)").bitcast(I32))
 
-        def deal(words, plane, name):
-            dealt_words = keep.tile([P, PACK, P], I32, name=name + "_dealt_words", align_bytes=64)
-            dealt_plane = keep.tile([P, PACK, P], U8, name=name + "_dealt_plane", align_bytes=64)
-            nc.vector.tensor_copy(out=dealt_words[:], in_=words[:].rearrange("p (m t) -> p t m", t=PACK))
-            nc.vector.tensor_copy(out=dealt_plane[:], in_=plane[:].rearrange("p (m t) -> p t m", t=PACK))
-            return dealt_words, dealt_plane
+        def deal(source, dtype, name):
+            dealt = keep.tile([P, PACK, P], dtype, name=name, align_bytes=64)
+            nc.vector.tensor_copy(out=dealt[:], in_=source[:].rearrange("p (m t) -> p t m", t=PACK))
+            return dealt
 
         x_plane = keep.tile([P, T], U8, name="x_plane", align_bytes=64)
         w1_plane = keep.tile([P, H], U8, name="w1_plane", tag="w_plane", align_bytes=64)
@@ -52,41 +50,53 @@ def tile_picked_softdtw_none_po_kernel(
         nc.gpsimd.memset(w1_plane[:].bitcast(I32), 0)
 
         lists = {}
-        for name, source in (("offs", offs), ("di", di), ("dj", dj), ("dk", dk)):
+        for name in ("offs", "di", "dj", "dk"):
             lists[name] = keep.tile([P, S // 16], U16, name="list_" + name)
-            nc.sync.dma_start(lists[name][:], source)
-        load_scale_rows([nc.scalar] * 4, x_plane, x_scales)
         x_raw = keep.tile([P, T], I32, name="x_raw", tag="big_a", align_bytes=64)
-        load_words(x_raw, x_words)
         w1_raw = keep.tile([P, H], I32, name="w1_raw", tag="big_b", align_bytes=64)
+        for name, source in (("offs", offs), ("di", di), ("dj", dj), ("dk", dk)):
+            nc.sync.dma_start(lists[name][:], source)
         load_words(w1_raw, w1_words)
-        load_scale_rows([nc.sync, nc.sync, nc.gpsimd, nc.gpsimd], w1_plane, w1_scales)
+        load_words(x_raw, x_words)
+        load_scale_rows(nc.scalar, x_plane, x_scales, range(4))
+        load_scale_rows(nc.sync, w1_plane, w1_scales, range(3))
+        load_scale_rows(nc.gpsimd, w1_plane, w1_scales, (3,))
         gain = keep.tile([P, PACK], F32, name="gain")
         nc.gpsimd.dma_start(out=gain[:], in_=gn.rearrange("(p t) o -> p (t o)", t=PACK))
 
         ident = keep.tile([P, P], F32, name="ident")
         make_identity(nc, ident[:])
 
-        warm = keep.tile([P, 1], F32, name="warm")
-        nc.scalar.activation(out=warm[:], in_=ident[:, 0:1], func=ACT.Exp)
+        ones = keep.tile([P, 2], F32, name="ones")
 
-        w1_dealt, w1_dealt_plane = deal(w1_raw, w1_plane, "w1")
+        def make_one(chunk, after):
+            nc.scalar.activation(out=ones[:, chunk : chunk + 1], in_=after[:, 0:1], func=ACT.Exp, scale=0.0)
 
-        w2_plane = keep.tile([P, N], U8, name="w2_plane", tag="w_plane", align_bytes=64)
-        nc.gpsimd.memset(w2_plane[:].bitcast(I32), 0)
-        w2_raw = keep.tile([P, N], I32, name="w2_raw", tag="big_b", align_bytes=64)
-        load_words(w2_raw, w2_words)
-        load_scale_rows([nc.sync] * 4, w2_plane, w2_scales)
+        make_one(0, ident)
+
+        w1_dealt = deal(w1_raw, I32, "w1_dealt")
 
         picked_plane = keep.tile([P, S], U8, name="picked_plane", align_bytes=64)
         nc.vector.tensor_copy(out=picked_plane[:], in_=x_plane[:].indirect(lists["offs"][:]))
         picked_words = keep.tile([P, S], U32, name="picked_words", align_bytes=64)
         half = S // 2
-        for h in range(2):
+
+        def pick_words(h):
             nc.vector.tensor_copy(
                 out=picked_words[:, h * half : (h + 1) * half],
                 in_=x_raw[:].bitcast(U32).indirect(lists["offs"][:, h * half // 16 : (h + 1) * half // 16]),
             )
+
+        pick_words(0)
+        w1_dealt_plane = deal(w1_plane, U8, "w1_dealt_plane")
+        pick_words(1)
+
+        w2_plane = keep.tile([P, N], U8, name="w2_plane", tag="w_plane", align_bytes=64)
+        nc.gpsimd.memset(w2_plane[:].bitcast(I32), 0)
+        w2_raw = keep.tile([P, N], I32, name="w2_raw", tag="big_b", align_bytes=64)
+        load_words(w2_raw, w2_words)
+        load_scale_rows(nc.sync, w2_plane, w2_scales, range(4))
+
 
         y = []
         for t in range(PACK):
@@ -106,7 +116,8 @@ def tile_picked_softdtw_none_po_kernel(
             nc.scalar.copy(out=window[:], in_=bank[:])
             y.append(window)
 
-        w2_dealt, w2_dealt_plane = deal(w2_raw, w2_plane, "w2")
+        w2_dealt = deal(w2_raw, I32, "w2_dealt")
+        w2_dealt_plane = deal(w2_plane, U8, "w2_dealt_plane")
 
         cost = keep.tile([P, PACK, S], F32, name="cost", tag="big_a", align_bytes=64)
         nc.sync.dma_start(out=cost[:], in_=cst.rearrange("(p t) j -> p t j", t=PACK))
@@ -126,83 +137,105 @@ def tile_picked_softdtw_none_po_kernel(
         out_plane = keep.tile([P, S], U8, name="out_plane", align_bytes=64)
         out_rows = out_0.rearrange("(p t) j -> p t j", t=PACK)
 
-        def add_transposed(bank, term, cols, slots, first=False, last=False):
-            for t in range(slots.start, slots.stop):
+        def add_transposed(bank, terms, cols, opens=False, closes=False):
+            for n, (term, t) in enumerate(terms):
                 nc.tensor.matmul(
                     bank[:, t, :], term[:, t, cols], ident[:],
-                    start=(first and t == 0), stop=(last and t == PACK - 1), is_transpose=True,
+                    start=(opens and n == 0), stop=(closes and n == len(terms) - 1), is_transpose=True,
                 )
 
-        def look_up(lo, hi):
-            width = hi - lo
-            names = ("first", "step", "low", "third", "gap", "gap3", "far", "near_w", "far_w")
-            v = {name: ring.tile([P, PACK, width], F32, name=name) for name in names}
-            cols = slice(lo // 16, hi // 16)
-            pairs = (slice(0, 2), slice(2, 4))
-            blocks = [slice(j, j + BLOCK) for j in range(0, width, BLOCK)]
+        width = S // 2
+        vector_work = keep.tile([P, 3, PACK, width], F32, name="vector_work")
+        scalar_work = keep.tile([P, 3, PACK, width], F32, name="scalar_work")
+        pairs = (slice(0, 2), slice(2, 4))
+        blocks = [slice(j, j + BLOCK) for j in range(0, width, BLOCK)]
+
+        def slots(term, s=slice(0, PACK)):
+            return [(term, t) for t in range(s.start, s.stop)]
+
+        def look_up(chunk):
+            lo = chunk * width
+            first, third = vector_work[:, chunk, :, :], vector_work[:, chunk + 1, :, :]
+            planes = [scalar_work[:, n, :, :] for n in range(3)]
+            gap, near_w, far_w = planes if chunk == 0 else (planes[2], planes[0], planes[1])
+            step = ring.tile([P, PACK, width], F32, name="step")
+            low = ring.tile([P, PACK, width], F32, name="low")
+            far = ring.tile([P, PACK, width], F32, name="far")
+            cols = slice(lo // 16, (lo + width) // 16)
             bases = [psum.tile([P, PACK, P], F32, name="base", tag="base") for b in blocks]
             sums = [psum.tile([P, PACK, P], F32, name="sums", tag="short") for b in blocks]
             for base, b in zip(bases, blocks):
-                add_transposed(base, cost[:, :, lo:hi], b, slice(0, PACK), first=True)
+                add_transposed(base, slots(cost[:, :, lo : lo + width]), b, opens=True)
             for t in range(PACK):
-                nc.vector.tensor_copy(out=v["first"][:, t, :], in_=y[t][:].indirect(lists["di"][:, cols]))
+                nc.vector.tensor_copy(out=first[:, t, :], in_=y[t][:].indirect(lists["di"][:, cols]))
             for t in range(PACK):
-                nc.vector.tensor_tensor(v["step"][:, t, :], y[t][:].indirect(lists["dj"][:, cols]), v["first"][:, t, :], ALU.subtract)
+                nc.vector.tensor_tensor(step[:, t, :], y[t][:].indirect(lists["dj"][:, cols]), first[:, t, :], ALU.subtract)
             for s in pairs:
-                nc.vector.scalar_tensor_tensor(v["low"][:, s, :], v["step"][:, s, :], 0.0, v["first"][:, s, :], ALU.min, ALU.add)
-                nc.scalar.activation(out=v["gap"][:, s, :], in_=v["step"][:, s, :], func=ACT.Abs)
-                for base, b in zip(bases, blocks):
-                    add_transposed(base, v["low"], b, s)
-                    add_transposed(base, v["gap"], b, s)
+                nc.vector.scalar_tensor_tensor(low[:, s, :], step[:, s, :], 0.0, first[:, s, :], ALU.min, ALU.add)
+            nc.scalar.activation(out=gap, in_=step[:], func=ACT.Abs)
+            for base, b in zip(bases, blocks):
+                add_transposed(base, slots(gap) + slots(low), b)
             for t in range(PACK):
-                nc.vector.tensor_tensor(v["third"][:, t, :], y[t][:].indirect(lists["dk"][:, cols]), v["low"][:, t, :], ALU.subtract)
+                nc.vector.tensor_tensor(third[:, t, :], y[t][:].indirect(lists["dk"][:, cols]), low[:, t, :], ALU.subtract)
             for s in pairs:
-                nc.vector.scalar_tensor_tensor(v["far"][:, s, :], v["third"][:, s, :], 0.0, v["gap"][:, s, :], ALU.min, ALU.subtract)
-                nc.scalar.activation(out=v["gap3"][:, s, :], in_=v["third"][:, s, :], func=ACT.Abs)
-                nc.scalar.activation(out=v["near_w"][:, s, :], in_=v["gap3"][:, s, :], func=ACT.Exp, scale=-1.0)
-                nc.scalar.activation(out=v["far_w"][:, s, :], in_=v["far"][:, s, :], func=ACT.Exp)
-                for bank, b in zip(sums, blocks):
-                    add_transposed(bank, v["near_w"], b, s, first=True)
-                for bank, b in zip(sums, blocks):
-                    add_transposed(bank, v["far_w"], b, s, last=True)
-                for base, b in zip(bases, blocks):
-                    add_transposed(base, v["far"], b, s, last=True)
-            return bases, sums
+                nc.vector.scalar_tensor_tensor(far[:, s, :], third[:, s, :], 0.0, gap[:, s, :], ALU.min, ALU.subtract)
 
-        def log_sums(lo, bases, sums):
+            def near(s, scratch, opens=False):
+                nc.scalar.activation(out=near_w[:, s, :], in_=scratch, func=ACT.Exp, scale=-1.0)
+                add_transposed(sums[0], slots(near_w, s), blocks[0], opens=opens)
+
+            def far_weight(s, closes=False):
+                nc.scalar.activation(out=far_w[:, s, :], in_=far[:, s, :], func=ACT.Exp)
+                add_transposed(sums[0], slots(far_w, s), blocks[0], closes=closes)
+
+            nc.scalar.activation(out=far_w[:, 1:3, :], in_=third[:, 0:2, :], func=ACT.Abs)
+            near(pairs[0], far_w[:, 1:3, :], opens=True)
+            nc.scalar.activation(out=far_w[:, 1:2, :], in_=third[:, 2:3, :], func=ACT.Abs)
+            near(slice(2, 3), far_w[:, 1:2, :])
+            nc.scalar.activation(out=far_w[:, 2:3, :], in_=third[:, 3:4, :], func=ACT.Abs)
+            far_weight(pairs[0])
+            near(slice(3, 4), far_w[:, 2:3, :])
+            far_weight(pairs[1], closes=True)
+            for base, b in zip(bases, blocks):
+                add_transposed(base, slots(far), b, closes=True)
+            add_transposed(sums[1], slots(far_w)[::-1] + slots(near_w), blocks[1], opens=True, closes=True)
             pieces = []
-            for n, (base, bank) in enumerate(zip(bases, sums)):
+            for base, bank in zip(bases, sums):
                 logs = ring.tile([P, H], F32, name="logs", bufs=4)
                 nc.scalar.activation(
                     out=logs[:].rearrange("j (u p e) -> j u p e", u=2, e=2),
                     in_=bank[:].rearrange("j (u e) p -> j u p e", u=2),
                     func=ACT.Ln,
-                    bias=1.0,
+                    bias=ones[:, chunk : chunk + 1],
                 )
-                pieces.append((lo + n * BLOCK, base, logs))
+                pieces.append((base, logs))
+            if chunk == 0:
+                make_one(1, pieces[0][1])
             return pieces
 
-        def second_layer(j0, base, logs):
-            cols = slice(j0, j0 + BLOCK)
-            soft = ring.tile([P, H], F32, name="soft")
+        def make_z(n, base, logs, soft):
             nc.vector.tensor_tensor(
-                soft[:].rearrange("j (u p e) -> j u p e", u=2, e=2),
+                soft.rearrange("j (u p e) -> j u p e", u=2, e=2),
                 base[:].rearrange("j (u e) p -> j u p e", u=2),
                 logs[:].rearrange("j (u p e) -> j u p e", u=2, e=2),
                 ALU.subtract,
             )
-            z_rows = ring.tile([P, H], BF16, name="z_rows")
-            nc.vector.tensor_tensor(z_rows[:], soft[:], gain_row[:], ALU.mult)
+            z_rows = ring.tile([P, H], BF16, name="z_rows", bufs=4)
+            nc.vector.tensor_tensor(z_rows[:], soft, gain_row[:], ALU.mult)
             pair_bank = psum.tile([P, 2, BLOCK], F32, name="pair_bank", tag="short")
             for u in range(2):
                 nc.tensor.transpose(pair_bank[:, u, :], z_rows[:].bitcast(F32)[:, u * P : (u + 1) * P], ident[:])
-            z_grouped = ring.tile([P, BLOCK * PACK], BF16, name="z_grouped", align_bytes=64)
-            nc.scalar.copy(
+            z_grouped = ring.tile([P, BLOCK * PACK], BF16, name="z_grouped", align_bytes=64, bufs=4)
+            (nc.scalar.copy if "vvss"[n] == "s" else nc.vector.tensor_copy)(
                 out=z_grouped[:].bitcast(F32).rearrange("p (j u) -> p j u", u=2),
                 in_=pair_bank[:].rearrange("p u j -> p j u"),
             )
-            z_words = ring.tile([P, BLOCK], U32, name="z_words", align_bytes=64)
-            z_plane = ring.tile([P, BLOCK], U8, name="z_plane", align_bytes=64)
+            return z_grouped
+
+        def second_layer(j0, z_grouped):
+            cols = slice(j0, j0 + BLOCK)
+            z_words = ring.tile([P, BLOCK], U32, name="z_words", align_bytes=64, bufs=4)
+            z_plane = ring.tile([P, BLOCK], U8, name="z_plane", align_bytes=64, bufs=4)
             nc.vector.quantize_mx(out=z_words[:].bitcast(FP8X4), scales=z_plane[:], in_=z_grouped[:])
             acc = psum.tile([P, PACK, BLOCK], F32, name="acc", tag="short")
             for t in range(PACK):
@@ -218,21 +251,21 @@ def tile_picked_softdtw_none_po_kernel(
             result = ring.tile([P, PACK, BLOCK], F32, name="result", bufs=4)
             nc.vector.tensor_tensor(result[:], acc[:], residual[:, :, cols], ALU.add)
             nc.sync.dma_start(out=out_rows[:, :, cols], in_=result[:])
-            grouped = ring.tile([P, BLOCK * PACK], BF16, name="grouped", align_bytes=64)
-            nc.scalar.copy(
+            grouped = ring.tile([P, BLOCK * PACK], BF16, name="grouped", align_bytes=64, bufs=4)
+            (nc.scalar.copy if "sssv"[j0 // BLOCK] == "s" else nc.vector.tensor_copy)(
                 out=grouped[:].rearrange("p (c i t) -> p c t i", i=4, t=PACK),
                 in_=result[:].rearrange("p t (c i) -> p c t i", i=4),
             )
             nc.vector.quantize_mx(out=out_words[:, cols].bitcast(FP8X4), scales=out_plane[:, cols], in_=grouped[:])
 
         words_out = out_1[0].rearrange("p n t -> p (n t)").bitcast(I32)
-        logged = []
-        for lo, hi in CHUNKS:
-            logged.append(log_sums(lo, *look_up(lo, hi)))
-        for (lo, hi), pieces in zip(CHUNKS, logged):
-            for piece in pieces:
-                second_layer(*piece)
-            nc.sync.dma_start(out=words_out[:, lo:hi], in_=out_words[:, lo:hi])
+        pieces = look_up(0) + look_up(1)
+        spare = vector_work[:].rearrange("p n (a t) j -> p (n a) (t j)", a=2)
+        grouped_z = [make_z(n, base, logs, spare[:, (4, 5, 2, 3)[n], :]) for n, (base, logs) in enumerate(pieces)]
+        for n in (0, 1, 2, 3):
+            second_layer(n * BLOCK, grouped_z[n])
+        for lo in (width, 0):
+            nc.sync.dma_start(out=words_out[:, lo : lo + width], in_=out_words[:, lo : lo + width])
         scale_rows = out_2[0].bitcast(I32)
         for q in range(4):
             queue = (nc.sync, nc.scalar)[q % 2]

@@ -45,7 +45,7 @@ def tile_picked_softdtw_none_po_kernel(
             return dealt
 
         x_plane = keep.tile([P, T], U8, name="x_plane", align_bytes=64)
-        w1_plane = keep.tile([P, H], U8, name="w1_plane", tag="w_plane", align_bytes=64)
+        w1_plane = keep.tile([P, H], U8, name="w1_plane", align_bytes=64)
         nc.vector.memset(x_plane[:].bitcast(I32), 0)
         nc.gpsimd.memset(w1_plane[:].bitcast(I32), 0)
 
@@ -91,18 +91,19 @@ def tile_picked_softdtw_none_po_kernel(
         w1_dealt_plane = deal(w1_plane, U8, "w1_dealt_plane")
         pick_words(1)
 
-        w2_plane = keep.tile([P, N], U8, name="w2_plane", tag="w_plane", align_bytes=64)
-        nc.gpsimd.memset(w2_plane[:].bitcast(I32), 0)
         w2_raw = keep.tile([P, N], I32, name="w2_raw", tag="big_b", align_bytes=64)
         load_words(w2_raw, w2_words)
-        load_scale_rows(nc.sync, w2_plane, w2_scales, range(4))
 
 
         y = []
         for t in range(PACK):
             bank = psum.tile([P, S], F32, name="y_bank", tag="short")
+            window = keep.tile([P, S], F32, name=f"y{t}")
             for h in range(2):
                 cols = slice(h * half, (h + 1) * half)
+                if t == 0 and h == 1:
+                    nc.scalar.copy(out=window[:, 0:half], in_=bank[:, 0:half])
+                    bank = psum.tile([P, S], F32, name="y_bank", tag="base")
                 nc.tensor.matmul_mx(
                     out=bank[:, cols],
                     lhsT=w1_dealt[:, t, :].bitcast(FP8X4),
@@ -112,12 +113,11 @@ def tile_picked_softdtw_none_po_kernel(
                     start=True,
                     stop=True,
                 )
-            window = keep.tile([P, S], F32, name=f"y{t}")
-            nc.scalar.copy(out=window[:], in_=bank[:])
+            rest = slice(half if t == 0 else 0, S)
+            nc.scalar.copy(out=window[:, rest], in_=bank[:, rest])
             y.append(window)
 
         w2_dealt = deal(w2_raw, I32, "w2_dealt")
-        w2_dealt_plane = deal(w2_plane, U8, "w2_dealt_plane")
 
         cost = keep.tile([P, PACK, S], F32, name="cost", tag="big_a", align_bytes=64)
         nc.sync.dma_start(out=cost[:], in_=cst.rearrange("(p t) j -> p t j", t=PACK))
@@ -146,7 +146,7 @@ def tile_picked_softdtw_none_po_kernel(
 
         width = S // 2
         vector_work = keep.tile([P, 3, PACK, width], F32, name="vector_work")
-        scalar_work = keep.tile([P, 3, PACK, width], F32, name="scalar_work")
+        scalar_work = keep.tile([P, 4, PACK, width], F32, name="scalar_work")
         pairs = (slice(0, 2), slice(2, 4))
         blocks = [slice(j, j + BLOCK) for j in range(0, width, BLOCK)]
 
@@ -157,24 +157,23 @@ def tile_picked_softdtw_none_po_kernel(
             lo = chunk * width
             first, third = vector_work[:, chunk, :, :], vector_work[:, chunk + 1, :, :]
             planes = [scalar_work[:, n, :, :] for n in range(3)]
-            gap, near_w, far_w = planes if chunk == 0 else (planes[2], planes[0], planes[1])
+            gap, near_w, far_w = planes
             step = ring.tile([P, PACK, width], F32, name="step")
             low = ring.tile([P, PACK, width], F32, name="low")
             far = ring.tile([P, PACK, width], F32, name="far")
             cols = slice(lo // 16, (lo + width) // 16)
             bases = [psum.tile([P, PACK, P], F32, name="base", tag="base") for b in blocks]
             sums = [psum.tile([P, PACK, P], F32, name="sums", tag="short") for b in blocks]
-            for base, b in zip(bases, blocks):
-                add_transposed(base, slots(cost[:, :, lo : lo + width]), b, opens=True)
             for t in range(PACK):
                 nc.vector.tensor_copy(out=first[:, t, :], in_=y[t][:].indirect(lists["di"][:, cols]))
             for t in range(PACK):
                 nc.vector.tensor_tensor(step[:, t, :], y[t][:].indirect(lists["dj"][:, cols]), first[:, t, :], ALU.subtract)
             for s in pairs:
                 nc.vector.scalar_tensor_tensor(low[:, s, :], step[:, s, :], 0.0, first[:, s, :], ALU.min, ALU.add)
-            nc.scalar.activation(out=gap, in_=step[:], func=ACT.Abs)
+            one = ones[:, chunk : chunk + 1]
+            nc.scalar.activation(out=gap, in_=step[:], func=ACT.Abs, scale=one)
             for base, b in zip(bases, blocks):
-                add_transposed(base, slots(gap) + slots(low), b)
+                add_transposed(base, slots(gap) + slots(low) + slots(cost[:, :, lo : lo + width]), b, opens=True)
             for t in range(PACK):
                 nc.vector.tensor_tensor(third[:, t, :], y[t][:].indirect(lists["dk"][:, cols]), low[:, t, :], ALU.subtract)
             for s in pairs:
@@ -182,26 +181,25 @@ def tile_picked_softdtw_none_po_kernel(
 
             def near(s, scratch, opens=False):
                 nc.scalar.activation(out=near_w[:, s, :], in_=scratch, func=ACT.Exp, scale=-1.0)
-                add_transposed(sums[0], slots(near_w, s), blocks[0], opens=opens)
+                for bank, b in zip(sums, blocks):
+                    add_transposed(bank, slots(near_w, s), b, opens=opens)
 
-            def far_weight(s, closes=False):
+            def far_weight(s, far_w, closes=False):
                 nc.scalar.activation(out=far_w[:, s, :], in_=far[:, s, :], func=ACT.Exp)
-                add_transposed(sums[0], slots(far_w, s), blocks[0], closes=closes)
+                for bank, b in zip(sums, blocks):
+                    add_transposed(bank, slots(far_w, s), b, closes=closes)
 
-            nc.scalar.activation(out=far_w[:, 1:3, :], in_=third[:, 0:2, :], func=ACT.Abs)
+            nc.scalar.activation(out=far_w[:, 1:3, :], in_=third[:, 0:2, :], func=ACT.Abs, scale=one)
             near(pairs[0], far_w[:, 1:3, :], opens=True)
-            nc.scalar.activation(out=far_w[:, 1:2, :], in_=third[:, 2:3, :], func=ACT.Abs)
-            near(slice(2, 3), far_w[:, 1:2, :])
-            nc.scalar.activation(out=far_w[:, 2:3, :], in_=third[:, 3:4, :], func=ACT.Abs)
-            far_weight(pairs[0])
-            near(slice(3, 4), far_w[:, 2:3, :])
-            far_weight(pairs[1], closes=True)
+            nc.scalar.activation(out=far_w[:, 2:4, :], in_=third[:, 2:4, :], func=ACT.Abs)
+            far_weight(pairs[0], far_w)
+            near(pairs[1], far_w[:, 2:4, :])
+            far_weight(pairs[1], scalar_work[:, 3, :, :], closes=True)
             for base, b in zip(bases, blocks):
                 add_transposed(base, slots(far), b, closes=True)
-            add_transposed(sums[1], slots(far_w)[::-1] + slots(near_w), blocks[1], opens=True, closes=True)
             pieces = []
             for base, bank in zip(bases, sums):
-                logs = ring.tile([P, H], F32, name="logs", bufs=4)
+                logs = ring.tile([P, H], F32, name="logs", bufs=4, align_bytes=64)
                 nc.scalar.activation(
                     out=logs[:].rearrange("j (u p e) -> j u p e", u=2, e=2),
                     in_=bank[:].rearrange("j (u e) p -> j u p e", u=2),
@@ -210,7 +208,7 @@ def tile_picked_softdtw_none_po_kernel(
                 )
                 pieces.append((base, logs))
             if chunk == 0:
-                make_one(1, pieces[0][1])
+                make_one(1, logs)
             return pieces
 
         def make_z(n, base, logs, soft):
@@ -225,9 +223,12 @@ def tile_picked_softdtw_none_po_kernel(
             pair_bank = psum.tile([P, 2, BLOCK], F32, name="pair_bank", tag="short")
             for u in range(2):
                 nc.tensor.transpose(pair_bank[:, u, :], z_rows[:].bitcast(F32)[:, u * P : (u + 1) * P], ident[:])
-            z_grouped = ring.tile([P, BLOCK * PACK], BF16, name="z_grouped", align_bytes=64, bufs=4)
-            (nc.scalar.copy if "vvss"[n] == "s" else nc.vector.tensor_copy)(
-                out=z_grouped[:].bitcast(F32).rearrange("p (j u) -> p j u", u=2),
+            return pair_bank
+
+        def regroup_z(n, pair_bank):
+            z_grouped = pieces[(0, 3, 2, 1)[n]][1][:, 0 : H // 2].bitcast(BF16)
+            (nc.scalar.copy if "vsss"[n] == "s" else nc.vector.tensor_copy)(
+                out=z_grouped.bitcast(F32).rearrange("p (j u) -> p j u", u=2),
                 in_=pair_bank[:].rearrange("p u j -> p j u"),
             )
             return z_grouped
@@ -236,7 +237,7 @@ def tile_picked_softdtw_none_po_kernel(
             cols = slice(j0, j0 + BLOCK)
             z_words = ring.tile([P, BLOCK], U32, name="z_words", align_bytes=64, bufs=4)
             z_plane = ring.tile([P, BLOCK], U8, name="z_plane", align_bytes=64, bufs=4)
-            nc.vector.quantize_mx(out=z_words[:].bitcast(FP8X4), scales=z_plane[:], in_=z_grouped[:])
+            nc.vector.quantize_mx(out=z_words[:].bitcast(FP8X4), scales=z_plane[:], in_=z_grouped)
             acc = psum.tile([P, PACK, BLOCK], F32, name="acc", tag="short")
             for t in range(PACK):
                 nc.tensor.matmul_mx(
@@ -248,20 +249,25 @@ def tile_picked_softdtw_none_po_kernel(
                     start=True,
                     stop=True,
                 )
-            result = ring.tile([P, PACK, BLOCK], F32, name="result", bufs=4)
-            nc.vector.tensor_tensor(result[:], acc[:], residual[:, :, cols], ALU.add)
-            nc.sync.dma_start(out=out_rows[:, :, cols], in_=result[:])
+            result = spare[:, (2, 3, 4, 5)[j0 // BLOCK], :].rearrange("p (t j) -> p t j", t=PACK)
+            nc.vector.tensor_tensor(result, acc[:], residual[:, :, cols], ALU.add)
+            nc.sync.dma_start(out=out_rows[:, :, cols], in_=result)
             grouped = ring.tile([P, BLOCK * PACK], BF16, name="grouped", align_bytes=64, bufs=4)
             (nc.scalar.copy if "sssv"[j0 // BLOCK] == "s" else nc.vector.tensor_copy)(
                 out=grouped[:].rearrange("p (c i t) -> p c t i", i=4, t=PACK),
-                in_=result[:].rearrange("p t (c i) -> p c t i", i=4),
+                in_=result.rearrange("p t (c i) -> p c t i", i=4),
             )
             nc.vector.quantize_mx(out=out_words[:, cols].bitcast(FP8X4), scales=out_plane[:, cols], in_=grouped[:])
 
         words_out = out_1[0].rearrange("p n t -> p (n t)").bitcast(I32)
         pieces = look_up(0) + look_up(1)
+        w2_plane = keep.tile([P, N], U8, name="w2_plane", tag="big_a", align_bytes=64)
+        nc.gpsimd.memset(w2_plane[:].bitcast(I32), 0)
+        load_scale_rows(nc.sync, w2_plane, w2_scales, range(4))
+        w2_dealt_plane = deal(w2_plane, U8, "w2_dealt_plane")
         spare = vector_work[:].rearrange("p n (a t) j -> p (n a) (t j)", a=2)
-        grouped_z = [make_z(n, base, logs, spare[:, (4, 5, 2, 3)[n], :]) for n, (base, logs) in enumerate(pieces)]
+        pair_banks = [make_z(n, base, logs, spare[:, (4, 5, 2, 3)[n], :]) for n, (base, logs) in enumerate(pieces)]
+        grouped_z = {n: regroup_z(n, pair_banks[n]) for n in (0, 1, 2, 3)}
         for n in (0, 1, 2, 3):
             second_layer(n * BLOCK, grouped_z[n])
         for lo in (width, 0):

@@ -36,13 +36,19 @@ def tile_picked_softdtw_none_po_kernel(
             for q in quadrants:
                 queue.dma_start(out=plane[32 * q : 32 * q + 4, :].bitcast(I32), in_=rows[4 * q : 4 * q + 4, :])
 
-        def load_words(tile, words):
-            nc.sync.dma_start(out=tile[:], in_=words[0].rearrange("p n t -> p (n t)").bitcast(I32))
+        def load_words(tile, words, cols=slice(None)):
+            nc.sync.dma_start(out=tile[:, cols], in_=words[0].rearrange("p n t -> p (n t)").bitcast(I32)[:, cols])
 
-        def deal(source, dtype, name):
-            dealt = keep.tile([P, PACK, P], dtype, name=name, align_bytes=64)
-            nc.vector.tensor_copy(out=dealt[:], in_=source[:].rearrange("p (m t) -> p t m", t=PACK))
-            return dealt
+        def deal(dealt, source, s=slice(0, PACK)):
+            nc.vector.tensor_copy(
+                out=dealt[:].rearrange("p t (m i) -> p m t i", i=4)[:, :, s, :],
+                in_=source[:].rearrange("p (m i t) -> p m t i", i=4, t=PACK)[:, :, s, :],
+            )
+
+        w1_dealt = keep.tile([P, PACK, P], I32, name="w1_dealt", align_bytes=64)
+        w1_dealt_plane = keep.tile([P, PACK, P], U8, name="w1_dealt_plane", align_bytes=64)
+        w2_dealt = keep.tile([P, PACK, P], I32, name="w2_dealt", align_bytes=64)
+        w2_dealt_plane = keep.tile([P, PACK, P], U8, name="w2_dealt_plane", align_bytes=64)
 
         x_plane = keep.tile([P, T], U8, name="x_plane", align_bytes=64)
         w1_plane = keep.tile([P, H], U8, name="w1_plane", align_bytes=64)
@@ -57,12 +63,11 @@ def tile_picked_softdtw_none_po_kernel(
         for name, source in (("offs", offs), ("di", di), ("dj", dj), ("dk", dk)):
             nc.sync.dma_start(lists[name][:], source)
         load_words(w1_raw, w1_words)
-        load_words(x_raw, x_words)
+        load_words(x_raw, x_words, slice(0, T // 2))
         load_scale_rows(nc.scalar, x_plane, x_scales, range(4))
-        load_scale_rows(nc.sync, w1_plane, w1_scales, range(3))
-        load_scale_rows(nc.gpsimd, w1_plane, w1_scales, (3,))
-        gain = keep.tile([P, PACK], F32, name="gain")
-        nc.gpsimd.dma_start(out=gain[:], in_=gn.rearrange("(p t) o -> p (t o)", t=PACK))
+        load_words(x_raw, x_words, slice(T // 2, T))
+        load_scale_rows(nc.sync, w1_plane, w1_scales, (0, 1))
+        load_scale_rows(nc.gpsimd, w1_plane, w1_scales, (2, 3))
 
         ident = keep.tile([P, P], F32, name="ident")
         make_identity(nc, ident[:])
@@ -74,7 +79,7 @@ def tile_picked_softdtw_none_po_kernel(
 
         make_one(0, ident)
 
-        w1_dealt = deal(w1_raw, I32, "w1_dealt")
+        deal(w1_dealt, w1_raw)
 
         picked_plane = keep.tile([P, S], U8, name="picked_plane", align_bytes=64)
         nc.vector.tensor_copy(out=picked_plane[:], in_=x_plane[:].indirect(lists["offs"][:]))
@@ -88,10 +93,11 @@ def tile_picked_softdtw_none_po_kernel(
             )
 
         pick_words(0)
-        w1_dealt_plane = deal(w1_plane, U8, "w1_dealt_plane")
         pick_words(1)
+        deal(w1_dealt_plane, w1_plane, slice(0, 1))
+        deal(w1_dealt_plane, w1_plane, slice(1, PACK))
 
-        w2_raw = keep.tile([P, N], I32, name="w2_raw", tag="big_b", align_bytes=64)
+        w2_raw = keep.tile([P, N], I32, name="w2_raw", tag="x_plane", align_bytes=64)
         load_words(w2_raw, w2_words)
 
 
@@ -117,13 +123,15 @@ def tile_picked_softdtw_none_po_kernel(
             nc.scalar.copy(out=window[:, rest], in_=bank[:, rest])
             y.append(window)
 
-        w2_dealt = deal(w2_raw, I32, "w2_dealt")
+        deal(w2_dealt, w2_raw)
 
         cost = keep.tile([P, PACK, S], F32, name="cost", tag="big_a", align_bytes=64)
         nc.sync.dma_start(out=cost[:], in_=cst.rearrange("(p t) j -> p t j", t=PACK))
-        residual = keep.tile([P, PACK, S], F32, name="residual", tag="big_b", align_bytes=64)
+        residual = keep.tile([P, PACK, S], F32, name="residual", tag="x_plane", align_bytes=64)
         nc.sync.dma_start(out=residual[:], in_=res.rearrange("(p t) j -> p t j", t=PACK))
 
+        gain = keep.tile([P, PACK], F32, name="gain", tag="big_b", align_bytes=64)
+        nc.sync.dma_start(out=gain[:], in_=gn.rearrange("(p t) o -> p (t o)", t=PACK))
         gain_bank = psum.tile([P, PACK, P], F32, name="gain_bank", tag="base")
         for t in range(PACK):
             nc.tensor.transpose(gain_bank[:, t, :], gain[:, t : t + 1].to_broadcast([P, P]), ident[:])
@@ -164,6 +172,9 @@ def tile_picked_softdtw_none_po_kernel(
             cols = slice(lo // 16, (lo + width) // 16)
             bases = [psum.tile([P, PACK, P], F32, name="base", tag="base") for b in blocks]
             sums = [psum.tile([P, PACK, P], F32, name="sums", tag="short") for b in blocks]
+            costs = slots(cost[:, :, lo : lo + width])
+            for base, b in zip(bases, blocks):
+                add_transposed(base, costs[:-1], b, opens=True)
             for t in range(PACK):
                 nc.vector.tensor_copy(out=first[:, t, :], in_=y[t][:].indirect(lists["di"][:, cols]))
             for t in range(PACK):
@@ -173,7 +184,7 @@ def tile_picked_softdtw_none_po_kernel(
             one = ones[:, chunk : chunk + 1]
             nc.scalar.activation(out=gap, in_=step[:], func=ACT.Abs, scale=one)
             for base, b in zip(bases, blocks):
-                add_transposed(base, slots(gap) + slots(low) + slots(cost[:, :, lo : lo + width]), b, opens=True)
+                add_transposed(base, slots(gap) + costs[-1:] + slots(low), b)
             for t in range(PACK):
                 nc.vector.tensor_tensor(third[:, t, :], y[t][:].indirect(lists["dk"][:, cols]), low[:, t, :], ALU.subtract)
             for s in pairs:
@@ -254,8 +265,8 @@ def tile_picked_softdtw_none_po_kernel(
             nc.sync.dma_start(out=out_rows[:, :, cols], in_=result)
             grouped = ring.tile([P, BLOCK * PACK], BF16, name="grouped", align_bytes=64, bufs=4)
             (nc.scalar.copy if "sssv"[j0 // BLOCK] == "s" else nc.vector.tensor_copy)(
-                out=grouped[:].rearrange("p (c i t) -> p c t i", i=4, t=PACK),
-                in_=result.rearrange("p t (c i) -> p c t i", i=4),
+                out=grouped[:].rearrange("p (c t) -> p c t", t=PACK),
+                in_=result.rearrange("p t c -> p c t"),
             )
             nc.vector.quantize_mx(out=out_words[:, cols].bitcast(FP8X4), scales=out_plane[:, cols], in_=grouped[:])
 
@@ -264,7 +275,7 @@ def tile_picked_softdtw_none_po_kernel(
         w2_plane = keep.tile([P, N], U8, name="w2_plane", tag="big_a", align_bytes=64)
         nc.gpsimd.memset(w2_plane[:].bitcast(I32), 0)
         load_scale_rows(nc.sync, w2_plane, w2_scales, range(4))
-        w2_dealt_plane = deal(w2_plane, U8, "w2_dealt_plane")
+        deal(w2_dealt_plane, w2_plane)
         spare = vector_work[:].rearrange("p n (a t) j -> p (n a) (t j)", a=2)
         pair_banks = [make_z(n, base, logs, spare[:, (4, 5, 2, 3)[n], :]) for n, (base, logs) in enumerate(pieces)]
         grouped_z = {n: regroup_z(n, pair_banks[n]) for n in (0, 1, 2, 3)}

from contextlib import ExitStack

import concourse.mybir as mybir
from concourse.masks import make_identity

K, T, S, N, H = 512, 2048, 512, 512, 512
FLOPS = 2 * K * H * S + 2 * H * N * S

F32 = mybir.dt.float32
BF16 = mybir.dt.bfloat16
I32 = mybir.dt.int32
U32 = mybir.dt.uint32
U16 = mybir.dt.uint16
U8 = mybir.dt.uint8
FP8X4 = mybir.dt.float8_e4m3fn_x4
ALU = mybir.AluOpType
ACT = mybir.ActivationFunctionType

P = 128
PACK = 4
BLOCK = 128
CHUNKS = ((0, 256), (256, 512))


def tile_picked_softdtw_none_po_kernel(
    tc, x_words, x_scales, w1_words, w1_scales, cst, gn, w2_words, w2_scales, res, offs, di, dj, dk, out_0, out_1, out_2
):
    nc = tc.nc
    with ExitStack() as ctx:
        keep = ctx.enter_context(tc.tile_pool(name="keep", bufs=1))
        ring = ctx.enter_context(tc.tile_pool(name="ring", bufs=2))
        psum = ctx.enter_context(tc.psum_pool(name="psum", bufs=4))

        def load_scale_rows(queue, plane, scales, quadrants):
            rows = scales[0].bitcast(I32)
            for q in quadrants:
                queue.dma_start(out=plane[32 * q : 32 * q + 4, :].bitcast(I32), in_=rows[4 * q : 4 * q + 4, :])

        def load_words(tile, words, cols=slice(None)):
            nc.sync.dma_start(out=tile[:, cols], in_=words[0].rearrange("p n t -> p (n t)").bitcast(I32)[:, cols])

        def deal(dealt, source, s=slice(0, PACK)):
            nc.vector.tensor_copy(
                out=dealt[:].rearrange("p t (m i) -> p m t i", i=4)[:, :, s, :],
                in_=source[:].rearrange("p (m i t) -> p m t i", i=4, t=PACK)[:, :, s, :],
            )

        w1_dealt = keep.tile([P, PACK, P], I32, name="w1_dealt", align_bytes=64)
        w1_dealt_plane = keep.tile([P, PACK, P], U8, name="w1_dealt_plane", align_bytes=64)
        w2_dealt = keep.tile([P, PACK, P], I32, name="w2_dealt", align_bytes=64)
        w2_dealt_plane = keep.tile([P, PACK, P], U8, name="w2_dealt_plane", align_bytes=64)

        x_plane = keep.tile([P, T], U8, name="x_plane", align_bytes=64)
        w1_plane = keep.tile([P, H], U8, name="w1_plane", align_bytes=64)
        nc.vector.memset(x_plane[:].bitcast(I32), 0)
        nc.gpsimd.memset(w1_plane[:].bitcast(I32), 0)

        lists = {}
        for name in ("offs", "di", "dj", "dk"):
            lists[name] = keep.tile([P, S // 16], U16, name="list_" + name)
        x_raw = keep.tile([P, T], I32, name="x_raw", tag="big_a", align_bytes=64)
        w1_raw = keep.tile([P, H], I32, name="w1_raw", tag="big_b", align_bytes=64)
        for name, source in (("offs", offs), ("di", di), ("dj", dj), ("dk", dk)):
            nc.sync.dma_start(lists[name][:], source)
        load_words(w1_raw, w1_words)
        load_words(x_raw, x_words, slice(0, T // 2))
        load_scale_rows(nc.scalar, x_plane, x_scales, range(4))
        load_words(x_raw, x_words, slice(T // 2, T))
        load_scale_rows(nc.sync, w1_plane, w1_scales, (0, 1))
        load_scale_rows(nc.gpsimd, w1_plane, w1_scales, (2, 3))

        ident = keep.tile([P, P], F32, name="ident")
        make_identity(nc, ident[:])

        ones = keep.tile([P, 2], F32, name="ones")

        def make_one(chunk, after):
            nc.scalar.activation(out=ones[:, chunk : chunk + 1], in_=after[:, 0:1], func=ACT.Exp, scale=0.0)

        make_one(0, ident)

        deal(w1_dealt, w1_raw)

        picked_plane = keep.tile([P, S], U8, name="picked_plane", align_bytes=64)
        nc.vector.tensor_copy(out=picked_plane[:], in_=x_plane[:].indirect(lists["offs"][:]))
        picked_words = keep.tile([P, S], U32, name="picked_words", align_bytes=64)
        half = S // 2

        def pick_words(h):
            nc.vector.tensor_copy(
                out=picked_words[:, h * half : (h + 1) * half],
                in_=x_raw[:].bitcast(U32).indirect(lists["offs"][:, h * half // 16 : (h + 1) * half // 16]),
            )

        pick_words(0)
        pick_words(1)
        deal(w1_dealt_plane, w1_plane, slice(0, 1))
        deal(w1_dealt_plane, w1_plane, slice(1, PACK))

        w2_raw = keep.tile([P, N], I32, name="w2_raw", tag="x_plane", align_bytes=64)
        load_words(w2_raw, w2_words)


        y = []
        for t in range(PACK):
            bank = psum.tile([P, S], F32, name="y_bank", tag="short")
            window = keep.tile([P, S], F32, name=f"y{t}")
            for h in range(2):
                cols = slice(h * half, (h + 1) * half)
                if t == 0 and h == 1:
                    nc.scalar.copy(out=window[:, 0:half], in_=bank[:, 0:half])
                    bank = psum.tile([P, S], F32, name="y_bank", tag="base")
                nc.tensor.matmul_mx(
                    out=bank[:, cols],
                    lhsT=w1_dealt[:, t, :].bitcast(FP8X4),
                    lhsT_scale=w1_dealt_plane[:, t, :],
                    rhs=picked_words[:, cols].bitcast(FP8X4),
                    rhs_scale=picked_plane[:, cols],
                    start=True,
                    stop=True,
                )
            rest = slice(half if t == 0 else 0, S)
            nc.scalar.copy(out=window[:, rest], in_=bank[:, rest])
            y.append(window)

        deal(w2_dealt, w2_raw)

        cost = keep.tile([P, PACK, S], F32, name="cost", tag="big_a", align_bytes=64)
        nc.sync.dma_start(out=cost[:], in_=cst.rearrange("(p t) j -> p t j", t=PACK))
        residual = keep.tile([P, PACK, S], F32, name="residual", tag="x_plane", align_bytes=64)
        nc.sync.dma_start(out=residual[:], in_=res.rearrange("(p t) j -> p t j", t=PACK))

        gain = keep.tile([P, PACK], F32, name="gain", tag="big_b", align_bytes=64)
        nc.sync.dma_start(out=gain[:], in_=gn.rearrange("(p t) o -> p (t o)", t=PACK))
        gain_bank = psum.tile([P, PACK, P], F32, name="gain_bank", tag="base")
        for t in range(PACK):
            nc.tensor.transpose(gain_bank[:, t, :], gain[:, t : t + 1].to_broadcast([P, P]), ident[:])
        gain_row = keep.tile([P, H], F32, name="gain_row")
        nc.scalar.copy(
            out=gain_row[:].rearrange("j (u p e) -> j u p e", u=2, e=2),
            in_=gain_bank[:].rearrange("j (u e) p -> j u p e", u=2),
        )

        out_words = keep.tile([P, S], I32, name="out_words", align_bytes=64)
        out_plane = keep.tile([P, S], U8, name="out_plane", align_bytes=64)
        out_rows = out_0.rearrange("(p t) j -> p t j", t=PACK)

        def add_transposed(bank, terms, cols, opens=False, closes=False):
            for n, (term, t) in enumerate(terms):
                nc.tensor.matmul(
                    bank[:, t, :], term[:, t, cols], ident[:],
                    start=(opens and n == 0), stop=(closes and n == len(terms) - 1), is_transpose=True,
                )

        width = S // 2
        vector_work = keep.tile([P, 3, PACK, width], F32, name="vector_work")
        scalar_work = keep.tile([P, 4, PACK, width], F32, name="scalar_work")
        pairs = (slice(0, 2), slice(2, 4))
        blocks = [slice(j, j + BLOCK) for j in range(0, width, BLOCK)]

        def slots(term, s=slice(0, PACK)):
            return [(term, t) for t in range(s.start, s.stop)]

        def look_up(chunk):
            lo = chunk * width
            first, third = vector_work[:, chunk, :, :], vector_work[:, chunk + 1, :, :]
            planes = [scalar_work[:, n, :, :] for n in range(3)]
            gap, near_w, far_w = planes
            step = ring.tile([P, PACK, width], F32, name="step")
            low = ring.tile([P, PACK, width], F32, name="low")
            far = ring.tile([P, PACK, width], F32, name="far")
            cols = slice(lo // 16, (lo + width) // 16)
            bases = [psum.tile([P, PACK, P], F32, name="base", tag="base") for b in blocks]
            sums = [psum.tile([P, PACK, P], F32, name="sums", tag="short") for b in blocks]
            costs = slots(cost[:, :, lo : lo + width])
            for base, b in zip(bases, blocks):
                add_transposed(base, costs[:-1], b, opens=True)
            for t in range(PACK):
                nc.vector.tensor_copy(out=first[:, t, :], in_=y[t][:].indirect(lists["di"][:, cols]))
            for t in range(PACK):
                nc.vector.tensor_tensor(step[:, t, :], y[t][:].indirect(lists["dj"][:, cols]), first[:, t, :], ALU.subtract)
            for s in pairs:
                nc.vector.scalar_tensor_tensor(low[:, s, :], step[:, s, :], 0.0, first[:, s, :], ALU.min, ALU.add)
            one = ones[:, chunk : chunk + 1]
            nc.scalar.activation(out=gap, in_=step[:], func=ACT.Abs, scale=one)
            for base, b in zip(bases, blocks):
                add_transposed(base, slots(gap) + costs[-1:] + slots(low), b)
            for t in range(PACK):
                nc.vector.tensor_tensor(third[:, t, :], y[t][:].indirect(lists["dk"][:, cols]), low[:, t, :], ALU.subtract)
            for s in pairs:
                nc.vector.scalar_tensor_tensor(far[:, s, :], third[:, s, :], 0.0, gap[:, s, :], ALU.min, ALU.subtract)

            def near(s, scratch, opens=False):
                nc.scalar.activation(out=near_w[:, s, :], in_=scratch, func=ACT.Exp, scale=-1.0)
                for bank, b in zip(sums, blocks):
                    add_transposed(bank, slots(near_w, s), b, opens=opens)

            def far_weight(s, far_w, closes=False):
                nc.scalar.activation(out=far_w[:, s, :], in_=far[:, s, :], func=ACT.Exp)
                for bank, b in zip(sums, blocks):
                    add_transposed(bank, slots(far_w, s), b, closes=closes)

            nc.scalar.activation(out=far_w[:, 1:3, :], in_=third[:, 0:2, :], func=ACT.Abs, scale=one)
            near(pairs[0], far_w[:, 1:3, :], opens=True)
            nc.scalar.activation(out=far_w[:, 2:4, :], in_=third[:, 2:4, :], func=ACT.Abs)
            far_weight(pairs[0], far_w)
            near(pairs[1], far_w[:, 2:4, :])
            far_weight(pairs[1], scalar_work[:, 3, :, :], closes=True)
            for base, b in zip(bases, blocks):
                add_transposed(base, slots(far), b, closes=True)
            pieces = []
            for base, bank in zip(bases, sums):
                logs = ring.tile([P, H], F32, name="logs", bufs=4, align_bytes=64)
                nc.scalar.activation(
                    out=logs[:].rearrange("j (u p e) -> j u p e", u=2, e=2),
                    in_=bank[:].rearrange("j (u e) p -> j u p e", u=2),
                    func=ACT.Ln,
                    bias=ones[:, chunk : chunk + 1],
                )
                pieces.append((base, logs))
            if chunk == 0:
                make_one(1, logs)
            return pieces

        def make_z(n, base, logs, soft):
            nc.vector.tensor_tensor(
                soft.rearrange("j (u p e) -> j u p e", u=2, e=2),
                base[:].rearrange("j (u e) p -> j u p e", u=2),
                logs[:].rearrange("j (u p e) -> j u p e", u=2, e=2),
                ALU.subtract,
            )
            z_rows = ring.tile([P, H], BF16, name="z_rows", bufs=4)
            nc.vector.tensor_tensor(z_rows[:], soft, gain_row[:], ALU.mult)
            pair_bank = psum.tile([P, 2, BLOCK], F32, name="pair_bank", tag="short")
            for u in range(2):
                nc.tensor.transpose(pair_bank[:, u, :], z_rows[:].bitcast(F32)[:, u * P : (u + 1) * P], ident[:])
            return pair_bank

        def regroup_z(n, pair_bank):
            z_grouped = pieces[(0, 3, 2, 1)[n]][1][:, 0 : H // 2].bitcast(BF16)
            (nc.scalar.copy if "vsss"[n] == "s" else nc.vector.tensor_copy)(
                out=z_grouped.bitcast(F32).rearrange("p (j u) -> p j u", u=2),
                in_=pair_bank[:].rearrange("p u j -> p j u"),
            )
            return z_grouped

        def second_layer(j0, z_grouped):
            cols = slice(j0, j0 + BLOCK)
            z_words = ring.tile([P, BLOCK], U32, name="z_words", align_bytes=64, bufs=4)
            z_plane = ring.tile([P, BLOCK], U8, name="z_plane", align_bytes=64, bufs=4)
            nc.vector.quantize_mx(out=z_words[:].bitcast(FP8X4), scales=z_plane[:], in_=z_grouped)
            acc = psum.tile([P, PACK, BLOCK], F32, name="acc", tag="short")
            for t in range(PACK):
                nc.tensor.matmul_mx(
                    out=acc[:, t, :],
                    lhsT=w2_dealt[:, t, :].bitcast(FP8X4),
                    lhsT_scale=w2_dealt_plane[:, t, :],
                    rhs=z_words[:].bitcast(FP8X4),
                    rhs_scale=z_plane[:],
                    start=True,
                    stop=True,
                )
            result = spare[:, (2, 3, 4, 5)[j0 // BLOCK], :].rearrange("p (t j) -> p t j", t=PACK)
            nc.vector.tensor_tensor(result, acc[:], residual[:, :, cols], ALU.add)
            nc.sync.dma_start(out=out_rows[:, :, cols], in_=result)
            grouped = ring.tile([P, BLOCK * PACK], BF16, name="grouped", align_bytes=64, bufs=4)
            (nc.scalar.copy if "sssv"[j0 // BLOCK] == "s" else nc.vector.tensor_copy)(
                out=grouped[:].rearrange("p (c t) -> p c t", t=PACK),
                in_=result.rearrange("p t c -> p c t"),
            )
            nc.vector.quantize_mx(out=out_words[:, cols].bitcast(FP8X4), scales=out_plane[:, cols], in_=grouped[:])

        words_out = out_1[0].rearrange("p n t -> p (n t)").bitcast(I32)
        pieces = look_up(0) + look_up(1)
        w2_plane = keep.tile([P, N], U8, name="w2_plane", tag="big_a", align_bytes=64)
        nc.gpsimd.memset(w2_plane[:].bitcast(I32), 0)
        load_scale_rows(nc.sync, w2_plane, w2_scales, range(4))
        deal(w2_dealt_plane, w2_plane)
        spare = vector_work[:].rearrange("p n (a t) j -> p (n a) (t j)", a=2)
        pair_banks = [make_z(n, base, logs, spare[:, (4, 5, 2, 3)[n], :]) for n, (base, logs) in enumerate(pieces)]
        grouped_z = {n: regroup_z(n, pair_banks[n]) for n in (0, 1, 2, 3)}
        for n in (0, 1, 2, 3):
            second_layer(n * BLOCK, grouped_z[n])
        for lo in (width, 0):
            nc.sync.dma_start(out=words_out[:, lo : lo + width], in_=out_words[:, lo : lo + width])
        scale_rows = out_2[0].bitcast(I32)
        for q in range(4):
            queue = (nc.sync, nc.scalar)[q % 2]
            queue.dma_start(out=scale_rows[4 * q : 4 * q + 4, :], in_=out_plane[32 * q : 32 * q + 4, :].bitcast(I32))
